import numpy as np, ml_dtypes
CORES = [51,54,179,182]
N = 4
BF = ml_dtypes.bfloat16
C, S, M, B, LB, A, CL = 8, 2048, 32, 32, 5, 20, 255
def fold(p):
    p = np.asarray(p, np.int64)[..., None, None]; n = np.arange(M)[:, None]; b = np.arange(B)[None, :]
    return ((n * p + b * (p >> LB)) >> 8).reshape(p.shape[:-2] + (M * B,))
def bend(t, a):
    return t + ((a * (t >> 3) ** 2) >> 12)
def trials(rng, a, h):
    v = bend(np.arange(S, dtype=np.int64), a[..., None]); last = np.sum(np.maximum.accumulate(v, -1) < S, -1) - 1
    p = np.maximum(256 * (last + 1) * h // (64 * M), 256); room = last - fold(p)[..., -1]
    return p, rng.integers(0, room[..., None] + 1, (N, 8, N * C)), room
def given(x, p, a, de):
    return {"x": x.reshape(N, 16, C * S).astype(np.float32).astype(BF), "pa": np.stack([p, a], -1).astype(np.int32), "de": de.astype(np.int32)}
def setup_inputs(rng):
    a = rng.integers(-A, A + 1, (N, 8)); p, de, room = trials(rng, a, rng.integers(32, 58, (N, 8)))
    return given(rng.integers(0, 16, (N, 16, C, S)), p, a, de)
def setup_inputs_ends(rng):
    a = rng.permuted(np.tile(np.array([-A, -A, -1, 0, 0, 1, A, A]), (N, 1)), axis=1)
    h = rng.permuted(np.tile(np.array([0, 0, 20, 40, 40, 60, 64, 64]), (N, 1)), axis=1)
    p, de, room = trials(rng, a, h); far = rng.permuted(np.tile(np.arange(N * C) % 2, (N, 8, 1)), axis=2)
    return given(rng.integers(0, 16, (N, 16, C, S)), p, a, far * room[..., None])
def setup_inputs_brink(rng):
    a = rng.integers(-A, A + 1, (N, 8)); p, de, room = trials(rng, a, rng.integers(32, 58, (N, 8)))
    u = rng.integers(0, 8, (N, 16, C, S)); return given(8 + (u == 0) - 1 * (u == 1), p, a, de)
def setup_inputs_alike(rng):
    a = np.repeat(rng.integers(-A, A + 1, (N, 1)), 8, axis=1); p, de, room = trials(rng, a, np.repeat(rng.integers(16, 61, (N, 1)), 8, axis=1))
    q = rng.integers(0, N); de[q] = de[q, :1]; return given(rng.integers(0, 16, (N, 16, C, S)), p, a, de)
def setup_inputs_spread(rng):
    a = rng.integers(-A, A + 1, (N, 8)); p, de, room = trials(rng, a, rng.integers(1, 65, (N, 8)))
    v = rng.integers(0, 16, (N, 16, C, S)); m = rng.integers(0, 16, (N, 16, C, 1)); up = rng.permutation(np.arange(16) % 2).reshape(1, 16, 1, 1)
    v = np.where(up == 1, np.maximum(v, m), np.minimum(v, m)); k = rng.permutation(16)[:3]; v[:, k[:2]] = 15; v[:, k[2]] = 0
    return given(v, p, a, de)
def check_inputs(d):
    try:
        bad = []; x = np.asarray(d["x"]).astype(np.float32); pa = np.asarray(d["pa"]).astype(np.int64); de = np.asarray(d["de"]).astype(np.int64)
        if x.shape != (N, 16, C * S) or pa.shape != (N, 8, 2) or de.shape != (N, 8, N * C): return ["shapes"]
        if not (np.isfinite(x).all() and (x == np.floor(x)).all() and x.min() >= 0 and x.max() <= 15): bad.append("samples")
        if pa[..., 0].min() < 256: bad.append("periods")
        if np.abs(pa[..., 1]).max() > A: bad.append("accelerations")
        if de.min() < 0: bad.append("delays")
        t = fold(pa[..., 0])[:, :, None, :] + de[..., None]
        if t.min() < 0 or t.max() >= S: bad.append("times")
        s = bend(t, pa[..., 1][:, :, None, None])
        if s.min() < 0 or s.max() >= S: bad.append("places")
        return bad
    except Exception:
        return ["form"]
def reference(x, pa, de):
    v = x.astype(np.float32).astype(np.int64).reshape(N, 16, C, S); y = np.zeros((N, 8, 16, B), np.int64)
    for r in range(N):
        for g in range(8):
            fp = fold(pa[r, g, 0]); a = int(pa[r, g, 1]); tot = np.zeros((16, M * B), np.int64)
            for q in range(N):
                for c in range(C):
                    tot += v[q, :, c][:, bend(fp + int(de[r, g, C * q + c]), a)]
            y[r, g] = np.add.reduce(np.minimum(tot, CL).reshape(16, M, B), axis=1)
    return {"y": y.reshape(N, 128, B).astype(np.float32)}

@@ -1,0 +1,342 @@
+from concourse.bass import DstId, RemoteDMATransfer
+from concourse.mybir import AluOpType, ActivationFunctionType
+
+S = 2048
+H = S // 2
+MAGIC = 12582912.0
+EIGHTH = 0.125 - 2.0 ** -14
+
+SCRATCH = {
+    "win0": ("sbuf", [128, S], "bfloat16"),
+    "win1": ("sbuf", [128, S], "bfloat16"),
+    "win2": ("sbuf", [128, S], "bfloat16"),
+    "win3": ("sbuf", [128, S], "bfloat16"),
+    "gat": ("sbuf", [128, 32768], "bfloat16"),
+    "off": ("sbuf", [128, 8, 256], "uint16"),
+    "jw": ("sbuf", [128, 2048], "float32"),
+    "sh": ("sbuf", [128, 2048], "float16"),
+    "clip": ("sbuf", [128, 1024], "float16"),
+    "pai": ("sbuf", [128, 4], "int32"),
+    "paf": ("sbuf", [128, 4], "float32"),
+    "dei": ("sbuf", [128, 2], "int32"),
+    "def32": ("sbuf", [128, 2], "float32"),
+    "pm": ("sbuf", [128, 8], "int32"),
+    "pf": ("sbuf", [128, 8], "float32"),
+    "ioa": ("sbuf", [128, 128], "bfloat16"),
+    "iob": ("sbuf", [128, 128], "bfloat16"),
+    "ioc": ("sbuf", [128, 256], "bfloat16"),
+    "ident": ("sbuf", [128, 128], "float16"),
+    "e8": ("sbuf", [128, 128], "float32"),
+    "twos": ("sbuf", [128, 128], "float32"),
+    "big": ("sbuf", [128, 128], "bfloat16"),
+    "diaga": ("sbuf", [128, 8], "float32"),
+    "wsum": ("sbuf", [128, 240], "bfloat16"),
+    "sel": ("sbuf", [128, 256], "float16"),
+    "selj": ("sbuf", [128, 256], "float16"),
+    "zed": ("sbuf", [128, 512], "bfloat16"),
+    "zedj": ("sbuf", [128, 512], "float16"),
+    "xd": ("sbuf", [128, 4, 32], "float16"),
+    "bcol": ("sbuf", [128, 2], "float32"),
+    "n32": ("sbuf", [128, 32], "float32"),
+    "r28": ("sbuf", [128, 32], "float32"),
+    "bq": ("sbuf", [128, 2], "float32"),
+    "uu": ("sbuf", [128, 64], "float32"),
+    "ff": ("sbuf", [128, 64], "float16"),
+    "yo": ("sbuf", [128, 32], "float32"),
+    "acc0": ("psum", [128, 512], "float32"),
+    "acc1": ("psum", [128, 512], "float32"),
+    "t0": ("psum", [128, 512], "float32"),
+    "t1": ("psum", [128, 512], "float32"),
+    "t2": ("psum", [128, 512], "float32"),
+    "t3": ("psum", [128, 512], "float32"),
+    "s0": ("psum", [128, 512], "float32"),
+    "s1": ("psum", [128, 512], "float32"),
+}
+NEV = 110
+SEMAPHORES = ["arr1", "arr2a", "arr2b", "arr3", "sent"] + ["e%d" % i for i in range(NEV)]
+
+
+def bits(m):
+    return bin(m).count("1")
+
+
+def rank_program(g, core, T, topo):
+    rank = T.rank_of(core)
+    if rank is None:
+        return
+    op = AluOpType
+    fn = ActivationFunctionType
+    V, A, P, Y = g.vector, g.scalar, g.tensor, g.sync
+    queues = {"G": g, "V": V, "A": A, "P": P, "Y": Y}
+
+    others = [c for c in T.cores if c != core]
+    sib = [c for c in others if c in topo.cores_of(core)][0]
+    peer = [c for c in others if c != sib and topo.die(c) == topo.die(core)][0]
+    diag = [c for c in others if c != sib and c != peer][0]
+    src = [T.rank_of(c) for c in (core, sib, peer, diag)]
+    wins = [T.win0, T.win1, T.win2, T.win3]
+
+    count = [0]
+    seen = set()
+
+    def event():
+        ev = ["e%d" % count[0], 0]
+        count[0] += 1
+        return ev
+
+    def sig(inst, ev=None, n=1):
+        if ev is None:
+            ev = event()
+        inst.then_inc(T.sem[ev[0]], n)
+        ev[1] += n
+        return ev
+
+    def wait(q, *evs):
+        for ev in evs:
+            if (q, ev[0]) not in seen:
+                seen.add((q, ev[0]))
+                queues[q].wait_ge(T.sem[ev[0]], ev[1])
+
+    l_pa = sig(Y.dma_start(T.pai[0:8, 0:2], T.pa[:]), n=16)
+    l_de = sig(A.dma_start(T.dei[:], T.de[:]), n=16)
+    l_x = event()
+    for c in range(8):
+        q = Y if c % 2 == 0 else A
+        sig(q.dma_start(T.win0[16 * c:16 * c + 16, :], T.x[:, S * c:S * (c + 1)]), l_x, 16)
+
+    kw = {"allow_small_or_imprecise_dtypes": True}
+    g_p = sig(g.iota(T.pm[:, 4:5], [[0, 1]], 0, 1))
+    g_a = sig(g.iota(T.ioa[:], [[1, 128]], 0, 0, **kw))
+    g_b = sig(g.iota(T.iob[:], [[1, 8], [0, 16]], 0, 0, **kw))
+    g_c = sig(g.iota(T.ioc[:], [[16, 2], [0, 8], [1, 16]], 0, 0, **kw))
+
+    far = topo.mask(core, peer)
+    whole = topo.mask(core, sib)
+    near = whole & ~far
+    rs, ps = topo.addr(sib, core)
+    rp, pp = topo.addr(peer, core)
+    wait("G", l_x)
+    sent = 0
+    for h, name in ((0, "arr2a"), (1, "arr2b")):
+        cols = slice(h * H, (h + 1) * H)
+        g.remote_dma_fused([
+            RemoteDMATransfer(dst_ids=[DstId(rid=rp, pnc=pp)], dma_engine_mask=far, remote_sem=T.sem[name],
+                              src=T.win0[:, cols], dst=T.win2[:, cols]),
+            RemoteDMATransfer(dst_ids=[DstId(rid=rs, pnc=ps)], dma_engine_mask=near, remote_sem=T.sem.arr1,
+                              src=T.win0[:, cols], dst=T.win1[:, cols]),
+        ], local_sem=T.sem.sent)
+        sent += bits(far) + bits(near)
+    a1 = ["arr1", 2 * bits(near)]
+    a2a = ["arr2a", bits(far)]
+    a2b = ["arr2b", bits(far)]
+    a3 = ["arr3", bits(near) + bits(whole)]
+    for h, ev, m in ((0, a2a, near), (1, a2b, whole)):
+        cols = slice(h * H, (h + 1) * H)
+        wait("G", ev)
+        g.remote_dma(T.win3[:, cols], T.win2[:, cols], T.sem.arr3, T.sem.sent, ps, rs, m)
+        sent += bits(m)
+    g.wait_ge(T.sem.sent, sent)
+    ready = [[l_x], [a1], [a2a, a2b], [a3]]
+
+    c_two = sig(V.memset(T.twos[0:8, :], 2.0))
+    c_big = sig(V.memset(T.big[:], MAGIC / 4))
+    c_w0 = sig(V.memset(T.wsum[:], 0.0))
+    wait("V", g_p)
+    c_and = event()
+    for k, m in enumerate((15, 31, 28, 3)):
+        sig(V.tensor_scalar(T.pm[:, k:k + 1], T.pm[:, 4:5], m, None, op.bitwise_and), c_and)
+    wait("V", c_and)
+    c_pf = sig(V.tensor_copy(T.pf[:, 0:5], T.pm[:, 0:5]))
+    wait("V", c_pf, g_a)
+    c_r28 = sig(V.tensor_scalar(T.r28[:], T.ioa[:, 0:32], T.pf[:, 2:3], None, op.is_equal))
+    c_id = sig(V.tensor_scalar(T.ident[:], T.ioa[:], T.pf[:, 4:5], None, op.is_equal))
+    c_sm = event()
+    sig(V.tensor_scalar(T.bcol[:], T.ioa[:, 0:2], 16.0, T.pf[:, 0:1], op.mult, op.add), c_sm)
+    sig(V.tensor_scalar(T.n32[:], T.ioa[:, 0:32], 32.0, None, op.mult), c_sm)
+    wait("V", g_b)
+    c_e8 = sig(V.tensor_scalar(T.e8[0:8, :], T.iob[0:8, :], T.pf[0:8, 4:5], None, op.is_equal))
+
+    wait("A", g_a, c_r28)
+    c_z = event()
+    for gl in range(2):
+        for k in range(4):
+            m = 4 * gl + k
+            col = 16 * gl + 4 * src[k]
+            sig(A.activation(T.zed[:, 64 * m:64 * (m + 1)], T.ioa[:, 0:64], fn.Identity,
+                             bias=T.r28[:, col:col + 1], scale=0.0), c_z)
+
+    wait("V", l_pa)
+    d_and = sig(V.tensor_scalar(T.pai[0:8, 2:4], T.pai[0:8, 0:2], 0x7FE0, None, op.bitwise_and))
+    wait("V", d_and)
+    d_paf = sig(V.tensor_scalar(T.paf[0:8, :], T.pai[0:8, :], 2.0 ** -13, None, op.mult))
+    wait("V", l_de)
+    d_def = sig(V.tensor_copy(T.def32[:], T.dei[:]))
+    wait("P", c_e8, d_paf)
+    p_s0 = sig(P.matmul(T.s0[:, 0:4], T.e8[0:8, :], T.paf[0:8, :], True, True))
+    wait("V", d_def)
+    d_x = event()
+    for cl in range(2):
+        sig(V.tensor_scalar(T.xd[:, :, 16 * cl:16 * (cl + 1)], T.iob[:, 0:64], T.pf[:, 3:4], T.def32[:, cl:cl + 1],
+                            op.is_equal, op.mult), d_x)
+    wait("V", p_s0, c_sm)
+    d_bq = sig(V.tensor_scalar(T.bq[:], T.bcol[:], T.s0[:, 2:3], -0.5 + 2.0 ** -9, op.mult, op.add))
+    wait("V", c_z)
+    c_zj = sig(V.tensor_scalar(T.zedj[:], T.zed[:], EIGHTH, None, op.mult))
+    wait("V", d_bq)
+    d_u = event()
+    for bh in range(2):
+        sig(V.tensor_scalar(T.uu[:, bh:64:2], T.n32[:], T.s0[:, 0:1], T.bq[:, bh:bh + 1], op.mult, op.add), d_u)
+    wait("V", g_c)
+    c_slj = sig(V.tensor_scalar(T.selj[:], T.ioc[:], T.pf[:, 1:2], EIGHTH, op.is_equal, op.mult))
+    wait("V", d_u)
+    d_f = sig(V.tensor_scalar(T.ff[:], T.uu[:], MAGIC, MAGIC + 3.0, op.add, op.subtract))
+    wait("V", d_paf, c_id)
+    d_dia = sig(V.tensor_scalar(T.diaga[0:8, :], T.ident[0:8, 0:8], T.paf[0:8, 1:2], None, op.mult))
+    c_sel = sig(V.tensor_scalar(T.sel[:], T.ioc[:], T.pf[:, 1:2], None, op.is_equal))
+    wait("V", c_w0)
+    c_w = sig(V.tensor_scalar(T.wsum[:, 112:128], T.ioa[:, 0:16], T.pf[:, 0:1], None, op.is_equal))
+
+    jb = [T.t0, T.t1, T.acc0, T.acc1]
+    tb = [T.t2, T.t3, T.t0, T.t1]
+    blk = [slice(512 * i, 512 * (i + 1)) for i in range(4)]
+    e_j, e_w, e_s, e_t, e_add, e_off = {}, {}, {}, {}, {}, {}
+
+    def delays(bank, i, z):
+        rows = slice(32 * i, 32 * (i + 1))
+        P.matmul(bank[:], T.xd[rows, :, :], z[rows, :], True, False)
+
+    def folds(bank, i, s):
+        rows = slice(32 * i, 32 * (i + 1))
+        for m in range(8):
+            gl = m // 4
+            mm = P.matmul(bank[:, 64 * m:64 * (m + 1)], s[rows, 128 * gl:128 * (gl + 1)], T.ff[rows, :], False, False)
+        return mm
+
+    def make_j(i):
+        rows = slice(32 * i, 32 * (i + 1))
+        folds(jb[i], i, T.selj)
+        e_j[i] = sig(P.matmul(jb[i][:], T.big[rows, :], T.zed[rows, :], False, True))
+        wait("A", e_j[i])
+        e_w[i] = sig(A.activation(T.jw[:, blk[i]], jb[i][:], fn.Square, bias=-MAGIC))
+
+    def make_t(i):
+        e_t[i] = sig(folds(tb[i], i, T.sel))
+
+    def shift(i):
+        wait("V", p_s1, e_w[i])
+        e_s[i] = event()
+        for gl in range(2):
+            tr = 2 * i + gl
+            cols = slice(256 * tr, 256 * (tr + 1))
+            sig(V.tensor_scalar(T.sh[:, cols], T.jw[:, cols], T.s1[:, tr:tr + 1], 1535.5 + 2.0 ** -13,
+                                op.mult, op.add), e_s[i])
+
+    def add_shift(i):
+        wait("P", c_id, e_t[i], e_s[i])
+        e_add[i] = sig(P.matmul(tb[i][:], T.ident[:], T.sh[:, blk[i]], False, True))
+
+    def offsets(i):
+        wait("V", e_add[i])
+        e_off[i] = event()
+        for gl in range(2):
+            tr = 2 * i + gl
+            sig(V.tensor_scalar(T.off[:, :, 32 * tr:32 * (tr + 1)], tb[i][:, 256 * gl:256 * (gl + 1)], -1533.0, None,
+                                op.add), e_off[i])
+
+    wait("P", c_z, d_x)
+    delays(tb[0], 0, T.zed)
+    delays(tb[1], 1, T.zed)
+    wait("P", c_zj)
+    delays(jb[0], 0, T.zedj)
+    delays(jb[1], 1, T.zedj)
+    wait("P", c_slj, d_f, c_big)
+    make_j(0)
+    wait("P", c_two, d_dia)
+    p_s1 = sig(P.matmul(T.s1[:, 0:8], T.twos[0:8, :], T.diaga[0:8, :], True, True))
+    make_j(1)
+    wait("P", c_sel)
+    make_t(0)
+    delays(jb[2], 2, T.zedj)
+    make_j(2)
+    shift(0)
+    add_shift(0)
+    delays(jb[3], 3, T.zedj)
+    make_j(3)
+    make_t(1)
+    shift(1)
+    add_shift(1)
+    offsets(0)
+    delays(tb[2], 2, T.zed)
+    make_t(2)
+    shift(2)
+    add_shift(2)
+    offsets(1)
+    delays(tb[3], 3, T.zed)
+    make_t(3)
+    shift(3)
+    add_shift(3)
+    offsets(2)
+    offsets(3)
+
+    done = {}
+
+    def gather(q, ph, g0, g1):
+        wait(q, *ready[ph // 2])
+        wait(q, *[e_off[i] for i in range(g0 // 2, (g1 + 1) // 2)])
+        out = T.gat[:, 4096 * ph + 512 * g0:4096 * ph + 512 * g1]
+        picked = wins[ph // 2][:, 0:S].indirect(T.off[:, ph, 32 * g0:32 * g1])
+        if q == "A":
+            done[(ph, g0)] = sig(A.activation(out, picked, fn.Copy))
+        else:
+            done[(ph, g0)] = sig(V.tensor_copy(out, picked))
+
+    acc = [T.acc0, T.acc1]
+    left = [32, 32]
+    full = {}
+
+    def add_up(ph, g0, g1):
+        wait("P", c_w, done[(ph, g0)])
+        kh = ph % 2
+        for tr in range(g0, g1):
+            lo = 4096 * ph + 512 * tr
+            mm = P.matmul(acc[kh][:], T.wsum[:, 112 - 16 * tr:240 - 16 * tr], T.gat[:, lo:lo + 512],
+                          left[kh] == 32, left[kh] == 1)
+            left[kh] -= 1
+        if left[kh] == 0:
+            full[kh] = sig(mm)
+
+    clipped = {}
+
+    def clip(kh, lo, hi):
+        wait("V", full[kh])
+        clipped[(kh, lo)] = sig(V.tensor_scalar(T.clip[:, 512 * kh + lo:512 * kh + hi], acc[kh][:, lo:hi], 255.0, None,
+                                                op.min))
+
+    def over_pulses(kh, lo, hi):
+        wait("P", clipped[(kh, lo)])
+        for c0 in range(512 * kh + lo, 512 * kh + hi, 32):
+            mm = P.matmul(T.s0[:, 0:32], T.ident[:], T.clip[:, c0:c0 + 32], c0 == 0, c0 == 1024 - 32)
+        return mm
+
+    pieces = [("A", 0, 0, 2), ("A", 1, 0, 4), ("V", 0, 2, 8), ("A", 1, 4, 8),
+              ("V", 2, 0, 8), ("A", 3, 0, 8),
+              ("V", 4, 0, 4), ("A", 5, 0, 4), ("V", 4, 4, 8), ("A", 5, 4, 8),
+              ("V", 6, 0, 4), ("A", 6, 4, 8),
+              ("V", 7, 0, 2), ("V", 7, 2, 3), ("A", 7, 4, 6)]
+    for q, ph, g0, g1 in pieces:
+        gather(q, ph, g0, g1)
+        add_up(ph, g0, g1)
+    clip(0, 0, 512)
+    over_pulses(0, 0, 512)
+    for q, ph, g0, g1 in [("A", 7, 6, 7), ("V", 7, 3, 4), ("A", 7, 7, 8)]:
+        gather(q, ph, g0, g1)
+        add_up(ph, g0, g1)
+    clip(1, 0, 256)
+    clip(1, 256, 512)
+    over_pulses(1, 0, 256)
+    p_y = sig(over_pulses(1, 256, 512))
+    wait("V", p_y)
+    v_y = sig(V.tensor_copy(T.yo[:], T.s0[:, 0:32]))
+    wait("Y", v_y)
+    stored = sig(Y.dma_start(T.y[:], T.yo[:]), n=16)
+    wait("Y", stored)

@@ -1,59 +1,97 @@
+import numpy as np
 from concourse.bass import DstId, RemoteDMATransfer
 from concourse.mybir import AluOpType, ActivationFunctionType
 
 S = 2048
-H = S // 2
+AMAX = 20
 MAGIC = 12582912.0
-EIGHTH = 0.125 - 2.0 ** -14
+LIFT = 1536.0
+DROP = (2031, 2031, 2048, 2031)
+
+
+def pair_spans():
+    spans = {}
+    t = np.arange(S)
+    for a in range(-AMAX, AMAX + 1):
+        s = t + ((a * (t >> 3) ** 2) >> 12)
+        ok = (s >= 0) & (s < S)
+        for df in range(3):
+            both = ok[:S - df] & ok[df:]
+            s0 = s[:S - df][both]
+            d = s[df:][both] - s0
+            for v in range(int(d.min()), int(d.max()) + 1):
+                at = s0[d == v]
+                if len(at):
+                    lo, hi = spans.get(v, (S, 0))
+                    spans[v] = (min(lo, int(at.min())), max(hi, int(at.max()) + 1))
+    return spans
+
+
+SPANS = pair_spans()
+DMIN = min(SPANS)
+NSTEP = max(SPANS) - DMIN + 1
 
 SCRATCH = {
-    "win0": ("sbuf", [128, S], "bfloat16"),
-    "win1": ("sbuf", [128, S], "bfloat16"),
-    "win2": ("sbuf", [128, S], "bfloat16"),
-    "win3": ("sbuf", [128, S], "bfloat16"),
-    "gat": ("sbuf", [128, 32768], "bfloat16"),
-    "off": ("sbuf", [128, 8, 256], "uint16"),
-    "jw": ("sbuf", [128, 2048], "float32"),
-    "sh": ("sbuf", [128, 2048], "float16"),
-    "clip": ("sbuf", [128, 1024], "float16"),
+    "xs": ("sbuf", [128, S], "bfloat16"),
+    "pairs": ("sbuf", [128, NSTEP * S], "float32"),
+    "gat": ("sbuf", [128, 16384], "float16"),
+    "offl": ("sbuf", [128, 4, 256], "uint16"),
+    "offr": ("sbuf", [128, 3, 256], "uint16"),
+    "outp": ("sbuf", [128, 4, 512], "float16"),
+    "inp": ("sbuf", [128, 4, 512], "float16"),
+    "outr": ("sbuf", [128, 512], "float32"),
+    "inr": ("sbuf", [128, 512], "float32"),
+    "hx": ("sbuf", [128, 1024], "float16"),
+    "cle": ("sbuf", [128, 512], "float16"),
+    "clo": ("sbuf", [128, 512], "float16"),
+    "jw": ("sbuf", [128, 4, 16, 4, 8], "uint16"),
+    "sh": ("sbuf", [128, 32, 8, 8], "float16"),
     "pai": ("sbuf", [128, 4], "int32"),
     "paf": ("sbuf", [128, 4], "float32"),
     "dei": ("sbuf", [128, 2], "int32"),
-    "def32": ("sbuf", [128, 2], "float32"),
+    "dfj": ("sbuf", [128, 2], "float32"),
     "pm": ("sbuf", [128, 8], "int32"),
     "pf": ("sbuf", [128, 8], "float32"),
-    "ioa": ("sbuf", [128, 128], "bfloat16"),
-    "iob": ("sbuf", [128, 128], "bfloat16"),
-    "ioc": ("sbuf", [128, 256], "bfloat16"),
+    "ioa": ("sbuf", [128, 34], "bfloat16"),
+    "iob": ("sbuf", [128, 64], "bfloat16"),
+    "ioh": ("sbuf", [128, 128], "bfloat16"),
+    "ioz": ("sbuf", [128, 128], "bfloat16"),
+    "n32": ("sbuf", [128, 64], "float32"),
+    "c256": ("sbuf", [128, 128], "bfloat16"),
+    "fill": ("sbuf", [128, 3, 128], "float16"),
     "ident": ("sbuf", [128, 128], "float16"),
+    "id256": ("sbuf", [128, 128], "bfloat16"),
+    "id32": ("sbuf", [128, 128], "float32"),
+    "ida": ("sbuf", [128, 128], "float16"),
+    "idb": ("sbuf", [128, 128], "float16"),
     "e8": ("sbuf", [128, 128], "float32"),
-    "twos": ("sbuf", [128, 128], "float32"),
+    "sixteen": ("sbuf", [128, 128], "float32"),
     "big": ("sbuf", [128, 128], "bfloat16"),
     "diaga": ("sbuf", [128, 8], "float32"),
-    "wsum": ("sbuf", [128, 240], "bfloat16"),
-    "sel": ("sbuf", [128, 256], "float16"),
-    "selj": ("sbuf", [128, 256], "float16"),
-    "zed": ("sbuf", [128, 512], "bfloat16"),
-    "zedj": ("sbuf", [128, 512], "float16"),
-    "xd": ("sbuf", [128, 4, 32], "float16"),
+    "acol": ("sbuf", [128, 8], "float32"),
+    "wabs": ("sbuf", [128, 33], "float16"),
+    "wsel": ("sbuf", [128, 16], "float16"),
+    "wpos": ("sbuf", [128, 33], "float16"),
+    "wneg": ("sbuf", [128, 33], "float16"),
+    "sel": ("sbuf", [128, 4, 128], "float16"),
+    "sela": ("sbuf", [128, 4, 128], "float16"),
+    "zed": ("sbuf", [128, 4, 128], "float16"),
+    "zedt": ("sbuf", [128, 4, 128], "float16"),
+    "xdj": ("sbuf", [128, 4, 32], "float16"),
     "bcol": ("sbuf", [128, 2], "float32"),
-    "n32": ("sbuf", [128, 32], "float32"),
-    "r28": ("sbuf", [128, 32], "float32"),
     "bq": ("sbuf", [128, 2], "float32"),
-    "uu": ("sbuf", [128, 64], "float32"),
-    "ff": ("sbuf", [128, 64], "float16"),
+    "uu": ("sbuf", [128, 128], "float32"),
+    "ffj": ("sbuf", [128, 128], "float16"),
     "yo": ("sbuf", [128, 32], "float32"),
-    "acc0": ("psum", [128, 512], "float32"),
-    "acc1": ("psum", [128, 512], "float32"),
-    "t0": ("psum", [128, 512], "float32"),
-    "t1": ("psum", [128, 512], "float32"),
-    "t2": ("psum", [128, 512], "float32"),
-    "t3": ("psum", [128, 512], "float32"),
-    "s0": ("psum", [128, 512], "float32"),
-    "s1": ("psum", [128, 512], "float32"),
+    "yy": ("psum", [128, 2048], "float32"),
+    "ja": ("psum", [128, 32, 2, 8], "float32"),
+    "jb": ("psum", [128, 32, 2, 8], "float32"),
+    "tt": ("psum", [128, 8, 8, 8], "float32"),
+    "ss": ("psum", [128, 512], "float32"),
 }
-NEV = 110
-SEMAPHORES = ["arr1", "arr2a", "arr2b", "arr3", "sent"] + ["e%d" % i for i in range(NEV)]
+NEV = 140
+SEMAPHORES = (["list0", "list1", "list2", "part0", "part1", "part2", "part3", "raw0", "raw1", "sent"]
+              + ["e%d" % i for i in range(NEV)])
 
 
 def bits(m):
@@ -73,270 +111,447 @@ def rank_program(g, core, T, topo):
     sib = [c for c in others if c in topo.cores_of(core)][0]
     peer = [c for c in others if c != sib and topo.die(c) == topo.die(core)][0]
     diag = [c for c in others if c != sib and c != peer][0]
-    src = [T.rank_of(c) for c in (core, sib, peer, diag)]
-    wins = [T.win0, T.win1, T.win2, T.win3]
+    partner = [diag, peer, sib, core]
+    src = [T.rank_of(c) for c in partner]
 
     count = [0]
-    seen = set()
+    known = {q: set() for q in queues}
 
     def event():
-        ev = ["e%d" % count[0], 0]
+        ev = ["e%d" % count[0], 0, set()]
         count[0] += 1
         return ev
 
-    def sig(inst, ev=None, n=1):
+    def sig(q, inst, ev=None, n=1):
         if ev is None:
             ev = event()
         inst.then_inc(T.sem[ev[0]], n)
         ev[1] += n
+        ev[2].update(known[q])
         return ev
 
     def wait(q, *evs):
         for ev in evs:
-            if (q, ev[0]) not in seen:
-                seen.add((q, ev[0]))
+            if ev[0] not in known[q]:
                 queues[q].wait_ge(T.sem[ev[0]], ev[1])
+                known[q].add(ev[0])
+                known[q].update(ev[2])
 
-    l_pa = sig(Y.dma_start(T.pai[0:8, 0:2], T.pa[:]), n=16)
-    l_de = sig(A.dma_start(T.dei[:], T.de[:]), n=16)
+    def ts(out, in0, s1, s2, op0, op1=None, ev=None):
+        if op1 is None:
+            return sig("V", V.tensor_scalar(out, in0, s1, None, op0), ev)
+        return sig("V", V.tensor_scalar(out, in0, s1, s2, op0, op1), ev)
+
+    def act(out, in_, func, ev=None, **kw):
+        return sig("A", A.activation(out, in_, func, **kw), ev)
+
+    l_pa = sig("Y", Y.dma_start(T.pai[0:8, 0:2], T.pa[:]), n=16)
+    l_de = sig("A", A.dma_start(T.dei[:], T.de[:]), n=16)
     l_x = event()
     for c in range(8):
-        q = Y if c % 2 == 0 else A
-        sig(q.dma_start(T.win0[16 * c:16 * c + 16, :], T.x[:, S * c:S * (c + 1)]), l_x, 16)
+        q = "Y" if c % 2 == 0 else "A"
+        sig(q, queues[q].dma_start(T.xs[16 * c:16 * c + 16, :], T.x[:, S * c:S * (c + 1)]), l_x, 16)
 
+    c_16 = sig("V", V.memset(T.sixteen[0:8, :], 16.0))
+    c_256 = sig("V", V.memset(T.c256[:], 256.0))
+    c_big = sig("V", V.memset(T.big[:], MAGIC / 4))
     kw = {"allow_small_or_imprecise_dtypes": True}
-    g_p = sig(g.iota(T.pm[:, 4:5], [[0, 1]], 0, 1))
-    g_a = sig(g.iota(T.ioa[:], [[1, 128]], 0, 0, **kw))
-    g_b = sig(g.iota(T.iob[:], [[1, 8], [0, 16]], 0, 0, **kw))
-    g_c = sig(g.iota(T.ioc[:], [[16, 2], [0, 8], [1, 16]], 0, 0, **kw))
+    g_p = sig("G", g.iota(T.pm[:, 4:5], [[0, 1]], 0, 1))
+    g_h = sig("G", g.iota(T.ioh[:], [[0, 8], [1, 16]], 0, 0, **kw))
+    g_a = sig("G", g.iota(T.ioa[:], [[1, 34]], 0, 0, **kw))
+    wait("G", c_16)
+    c_e8 = sig("G", g.affine_select(T.e8[0:8, :], T.sixteen[0:8, :], [[-1, 8], [0, 16]], op.is_equal, 0.0, 0, 1))
+    g_z = sig("G", g.iota(T.ioz[:], [[0, 4], [16, 4], [0, 8]], 0, 0, **kw))
+    g_b = sig("G", g.iota(T.iob[:], [[1, 4], [0, 16]], 0, 0, **kw))
+    g_n = sig("G", g.iota(T.n32[:], [[0, 2], [32, 32]], 0, 0, **kw))
+    wait("G", c_256)
+    c_id256 = sig("G", g.affine_select(T.id256[:], T.c256[:], [[-1, 128]], op.is_equal, 0.0, 0, 1))
+
+    wait("V", g_p)
+    c_and = event()
+    for k, m in enumerate((15, 63, 60, 3)):
+        ts(T.pm[:, k:k + 1], T.pm[:, 4:5], m, None, op.bitwise_and, ev=c_and)
+    wait("V", c_and)
+    c_pf = sig("V", V.tensor_copy(T.pf[:, 0:5], T.pm[:, 0:5]))
+    p15, p63, p60, p3, pall = [T.pf[:, k:k + 1] for k in range(5)]
+    wait("V", c_pf, g_a)
+    c_b1 = ts(T.bcol[:], T.ioa[:, 0:2], p15, p15, op.add, op.add)
+    wait("V", g_h)
+    c_sel = event()
+    for k in range(4):
+        ts(T.sel[:, k, :], T.ioh[:], 16.0 * k, p63, op.add, op.is_equal, c_sel)
+    wait("V", g_z)
+    c_z = event()
+
+    def make_z(w):
+        ts(T.zed[:, w, :], T.ioz[:], 4.0 * src[w], p60, op.add, op.is_equal, c_z)
+
+    make_z(0)
+    make_z(1)
+    wait("V", l_pa)
+    d_and = ts(T.pai[0:8, 2:4], T.pai[0:8, 0:2], 0x7FE0, None, op.bitwise_and)
+    make_z(2)
+    wait("V", d_and)
+    d_paf = ts(T.paf[0:8, :], T.pai[0:8, :], 2.0 ** -20, None, op.mult)
+    wait("P", c_e8, d_paf)
+    p_s0 = sig("P", P.matmul(T.ss[:, 0:4], T.e8[0:8, :], T.paf[0:8, :], True, True))
+    make_z(3)
+    wait("V", l_de)
+    d_dfj = ts(T.dfj[:], T.dei[:], -1023.5, 0.125, op.add, op.mult)
+    wait("V", d_paf)
+    d_dia = ts(T.diaga[0:8, :], T.ioa[0:8, 0:8], T.pf[0:8, 4:5], T.paf[0:8, 1:2], op.is_equal, op.mult)
+    wait("V", p_s0, c_b1)
+    d_bq = ts(T.bq[:], T.bcol[:], T.ss[:, 2:3], (-0.5 + 2.0 ** -9) / 8, op.mult, op.add)
+    wait("V", d_dfj, g_b)
+    d_xj = event()
+    ts(T.xdj[:, :, 0:16], T.iob[:], p3, T.dfj[:, 0:1], op.is_equal, op.mult, d_xj)
+    wait("V", d_bq, g_n)
+    d_u = event()
+    for e in range(2):
+        ts(T.uu[:, 64 * e:64 * (e + 1)], T.n32[:], T.ss[:, 0:1], T.bq[:, e:e + 1], op.mult, op.add, d_u)
+    ts(T.xdj[:, :, 16:32], T.iob[:], p3, T.dfj[:, 1:2], op.is_equal, op.mult, d_xj)
+    wait("V", d_u)
+    d_f = ts(T.ffj[:], T.uu[:], MAGIC / 8, MAGIC / 8 + 0.5, op.add, op.subtract)
+
+    wait("A", c_256)
+    c_fill = event()
+    for k, v in enumerate((-2047.0 / 16384, 0.125, 1.0)):
+        act(T.fill[:, k, :], T.c256[:], fn.Copy, c_fill, scale=v / 256)
+    wait("A", c_b1)
+    c_abs = act(T.wabs[:], T.ioa[:, 0:33], fn.Abs, bias=T.bcol[:, 1:2], scale=-1.0)
+    wait("A", c_abs)
+    c_pos = act(T.wpos[:], T.wabs[:], fn.Relu, bias=1.0, scale=-1.0)
+    wait("A", c_pos)
+    c_w = act(T.wsel[:], T.wpos[:, 1:33:2], fn.Copy, scale=1.0 / 256)
+    act(T.wneg[:], T.wpos[:], fn.Copy, c_w, scale=-1.0)
+    wait("A", c_sel)
+    c_t = act(T.sela[:], T.sel[:], fn.Copy, scale=-2047.0 / 2048)
+    wait("A", c_z)
+    act(T.zedt[:], T.zed[:], fn.Copy, c_t, scale=2.0 ** -11)
+    wait("G", c_fill)
+    c_ab, c_late = event(), event()
+    for out, k, ev in ((T.ida, 0, c_ab), (T.idb, 1, c_ab), (T.ident, 2, c_late), (T.id32, 2, c_late)):
+        sig("G", g.affine_select(out[:], T.fill[:, k, :], [[-1, 128]], op.is_equal, 0.0, 0, 1), ev)
+
+    wait("P", d_dia)
+    p_s1 = sig("P", P.matmul(T.tt[:, 0, 0, :], T.sixteen[0:8, :], T.diaga[0:8, :], True, True))
+    p_y = {}
+
+    def make_y(k):
+        wait("P", l_x, c_id256)
+        p_y[k] = sig("P", P.matmul(T.yy[:, 512 * k:512 * (k + 1)], T.id256[:], T.xs[:, 512 * k:512 * (k + 1)],
+                                   True, True))
+
+    e_pairs = event()
+    free = {"ss": [d_u]}
+
+    def pairs_v(d, lo, hi):
+        wait("V", *[p_y[k] for k in range(lo // 512, (hi + 511) // 512)])
+        base = (d - DMIN) * S
+        sig("V", V.tensor_tensor(T.pairs[:, base + lo:base + hi], T.yy[:, lo:hi], T.xs[:, lo + d:hi + d], op.add),
+            e_pairs)
+
+    def pairs_a(lo, hi):
+        wait("A", l_x)
+        act(T.pairs[:, -DMIN * S + lo:-DMIN * S + hi], T.xs[:, lo:hi], fn.Copy, e_pairs, scale=257.0)
+
+    def pairs_p(d, lo, hi):
+        wait("P", c_late, *free["ss"])
+        P.matmul(T.ss[:, 0:hi - lo], T.id256[:], T.xs[:, lo:hi], True, False)
+        return d, lo, hi, sig("P", P.matmul(T.ss[:, 0:hi - lo], T.ident[:], T.xs[:, lo + d:hi + d], False, True))
+
+    copied = []
+
+    def pairs_copy(d, lo, hi, ev):
+        wait("A", ev)
+        base = (d - DMIN) * S
+        copied.append(act(T.pairs[:, base + lo:base + hi], T.ss[:, 0:hi - lo], fn.Copy))
+        free["ss"] = [copied[-1]]
+
+    jbank = [T.ja, T.jb]
+    e_j, e_sq, e_sh, e_t, e_add, e_off = {}, {}, {}, {}, {}, {}
+
+    def make_j(u, hh):
+        rows = slice(64 * hh, 64 * (hh + 1))
+        bank = jbank[hh]
+        z = T.zed[rows, 2 * u:2 * u + 2, :]
+        wait("P", c_z, d_xj)
+        if u:
+            wait("P", e_sq[(0, hh)])
+        for e in range(2):
+            P.matmul(bank[:, 16 * e:16 * (e + 1), :, :], T.xdj[rows, :, :], z, e == 0, False)
+        wait("P", c_sel, d_f, c_big)
+        for k in range(4):
+            P.matmul(bank[:, k // 2:32:2, k % 2, :], T.sel[rows, k, :], T.ffj[rows, :], False, False)
+        for e in range(2):
+            mm = P.matmul(bank[:, 16 * e:16 * (e + 1), :, :], T.big[rows, :], z, False, e == 1)
+        e_j[(u, hh)] = sig("P", mm)
+
+    def make_t(u, hh):
+        rows = slice(64 * hh, 64 * (hh + 1))
+        wait("P", c_t, e_off[0] if u else c_a)
+        if hh:
+            wait("P", e_t[(u, 0)])
+        P.matmul(T.tt[:, :, 4 * hh:4 * hh + 4, :], T.xdj[rows, :, :], T.zedt[rows, 2 * u:2 * u + 2, :], hh == 0, False)
+        for k in range(4):
+            for e, s in enumerate((T.sela, T.sel)):
+                mm = P.matmul(T.tt[:, :, 4 * hh + k, :], s[rows, k, :], T.ffj[rows, 64 * e:64 * (e + 1)], False, False)
+        e_t[(u, hh)] = sig("P", mm)
+
+    def square(u, hh):
+        wait("A", e_j[(u, hh)])
+        e_sq[(u, hh)] = act(T.jw[:, 2 * u + hh, :, :, :], jbank[hh][:], fn.Square, bias=128.0 - MAGIC)
+
+    def shift(q, u, hh):
+        wait(q, c_a, e_sq[(u, hh)])
+        if u not in e_sh:
+            e_sh[u] = event()
+        for k in range(4):
+            tr = 4 * hh + k
+            out, w, a = T.sh[:, 16 * u:16 * (u + 1), tr, :], T.jw[:, 2 * u + hh, :, k, :], T.acol[:, tr:tr + 1]
+            if q == "A":
+                act(out, w, fn.Identity, e_sh[u], bias=LIFT - 0.5 + 2.0 ** -13, scale=a)
+            else:
+                ts(out, w, a, LIFT - 0.5 + 2.0 ** -13, op.mult, op.add, e_sh[u])
+
+    def add_shift(u):
+        wait("P", c_ab, e_t[(u, 1)], e_sh[u])
+        P.matmul(T.tt[:], T.ida[:], T.sh[:, 16 * u:16 * u + 8, :, :], False, False)
+        e_add[u] = sig("P", P.matmul(T.tt[:], T.idb[:], T.sh[:, 16 * u + 8:16 * u + 16, :, :], False, True))
+
+    def offsets(u):
+        wait("A", e_add[u])
+        e_off[u] = act(T.offl[:, 2 * u:2 * u + 2, :], T.tt[:], fn.Identity, bias=-DMIN * S + 1027.5 - LIFT,
+                       scale=16384.0)
+
+    lo1, hi1 = SPANS[-1]
+    wait("A", p_s1)
+    c_a = act(T.acol[:], T.tt[:, 0, 0, :], fn.Copy, scale=16.0)
+    pairs_a(0, 1280)
+    make_y(0)
+    make_y(1)
+    make_j(0, 0)
+    make_j(0, 1)
+    pairs_v(1, 0, 1024)
+    pairs_v(2, 0, 448)
+    square(0, 0)
+    square(0, 1)
+    make_t(0, 0)
+    make_t(0, 1)
+    make_y(2)
+    make_y(3)
+    shift("V", 0, 0)
+    shift("A", 0, 1)
+    add_shift(0)
+    make_j(1, 0)
+    make_j(1, 1)
+    pairs_v(2, 448, 1024)
+    pairs_v(3, SPANS[3][0], 1024)
+    for d in sorted(SPANS):
+        if d not in (0, -1):
+            pairs_v(d, 1024 if d in (1, 2, 3) else SPANS[d][0], SPANS[d][1])
+    pairs_v(-1, lo1 + 1008, hi1)
+    pairs_a(1280, S)
+    offsets(0)
+    staged = pairs_p(-1, lo1, lo1 + 512)
+    square(1, 0)
+    shift("A", 1, 0)
+    square(1, 1)
+    make_t(1, 0)
+    make_t(1, 1)
+    pairs_copy(*staged)
+    staged = pairs_p(-1, lo1 + 512, lo1 + 1008)
+    shift("A", 1, 1)
+    add_shift(1)
+    pairs_copy(*staged)
+    offsets(1)
 
     far = topo.mask(core, peer)
     whole = topo.mask(core, sib)
     near = whole & ~far
-    rs, ps = topo.addr(sib, core)
-    rp, pp = topo.addr(peer, core)
-    wait("G", l_x)
-    sent = 0
-    for h, name in ((0, "arr2a"), (1, "arr2b")):
-        cols = slice(h * H, (h + 1) * H)
-        g.remote_dma_fused([
-            RemoteDMATransfer(dst_ids=[DstId(rid=rp, pnc=pp)], dma_engine_mask=far, remote_sem=T.sem[name],
-                              src=T.win0[:, cols], dst=T.win2[:, cols]),
-            RemoteDMATransfer(dst_ids=[DstId(rid=rs, pnc=ps)], dma_engine_mask=near, remote_sem=T.sem.arr1,
-                              src=T.win0[:, cols], dst=T.win1[:, cols]),
-        ], local_sem=T.sem.sent)
-        sent += bits(far) + bits(near)
-    a1 = ["arr1", 2 * bits(near)]
-    a2a = ["arr2a", bits(far)]
-    a2b = ["arr2b", bits(far)]
-    a3 = ["arr3", bits(near) + bits(whole)]
-    for h, ev, m in ((0, a2a, near), (1, a2b, whole)):
-        cols = slice(h * H, (h + 1) * H)
-        wait("G", ev)
-        g.remote_dma(T.win3[:, cols], T.win2[:, cols], T.sem.arr3, T.sem.sent, ps, rs, m)
-        sent += bits(m)
-    g.wait_ge(T.sem.sent, sent)
-    ready = [[l_x], [a1], [a2a, a2b], [a3]]
+    sent = [0]
 
-    c_two = sig(V.memset(T.twos[0:8, :], 2.0))
-    c_big = sig(V.memset(T.big[:], MAGIC / 4))
-    c_w0 = sig(V.memset(T.wsum[:], 0.0))
-    wait("V", g_p)
-    c_and = event()
-    for k, m in enumerate((15, 31, 28, 3)):
-        sig(V.tensor_scalar(T.pm[:, k:k + 1], T.pm[:, 4:5], m, None, op.bitwise_and), c_and)
-    wait("V", c_and)
-    c_pf = sig(V.tensor_copy(T.pf[:, 0:5], T.pm[:, 0:5]))
-    wait("V", c_pf, g_a)
-    c_r28 = sig(V.tensor_scalar(T.r28[:], T.ioa[:, 0:32], T.pf[:, 2:3], None, op.is_equal))
-    c_id = sig(V.tensor_scalar(T.ident[:], T.ioa[:], T.pf[:, 4:5], None, op.is_equal))
-    c_sm = event()
-    sig(V.tensor_scalar(T.bcol[:], T.ioa[:, 0:2], 16.0, T.pf[:, 0:1], op.mult, op.add), c_sm)
-    sig(V.tensor_scalar(T.n32[:], T.ioa[:, 0:32], 32.0, None, op.mult), c_sm)
-    wait("V", g_b)
-    c_e8 = sig(V.tensor_scalar(T.e8[0:8, :], T.iob[0:8, :], T.pf[0:8, 4:5], None, op.is_equal))
+    def send(k, dst, source, sem, mask):
+        r, p = topo.addr(partner[k], core)
+        g.remote_dma(dst, source, T.sem[sem], T.sem.sent, p, r, mask)
+        sent[0] += bits(mask)
 
-    wait("A", g_a, c_r28)
-    c_z = event()
-    for gl in range(2):
-        for k in range(4):
-            m = 4 * gl + k
-            col = 16 * gl + 4 * src[k]
-            sig(A.activation(T.zed[:, 64 * m:64 * (m + 1)], T.ioa[:, 0:64], fn.Identity,
-                             bias=T.r28[:, col:col + 1], scale=0.0), c_z)
+    for k, mask in enumerate((far, far, near)):
+        wait("G", e_off[k // 2])
+        send(k, T.offr[:, k, :], T.offl[:, k, :], "list%d" % k, mask)
+    lists = [["list0", bits(far), set()], ["list1", bits(far), set()], ["list2", bits(near), set()], e_off[1]]
+    parts = [["part%d" % i, bits(far), set()] for i in range(4)]
+    raws = [["raw%d" % k, bits(whole), set()] for k in range(2)]
 
-    wait("V", l_pa)
-    d_and = sig(V.tensor_scalar(T.pai[0:8, 2:4], T.pai[0:8, 0:2], 0x7FE0, None, op.bitwise_and))
-    wait("V", d_and)
-    d_paf = sig(V.tensor_scalar(T.paf[0:8, :], T.pai[0:8, :], 2.0 ** -13, None, op.mult))
-    wait("V", l_de)
-    d_def = sig(V.tensor_copy(T.def32[:], T.dei[:]))
-    wait("P", c_e8, d_paf)
-    p_s0 = sig(P.matmul(T.s0[:, 0:4], T.e8[0:8, :], T.paf[0:8, :], True, True))
-    wait("V", d_def)
-    d_x = event()
-    for cl in range(2):
-        sig(V.tensor_scalar(T.xd[:, :, 16 * cl:16 * (cl + 1)], T.iob[:, 0:64], T.pf[:, 3:4], T.def32[:, cl:cl + 1],
-                            op.is_equal, op.mult), d_x)
-    wait("V", p_s0, c_sm)
-    d_bq = sig(V.tensor_scalar(T.bq[:], T.bcol[:], T.s0[:, 2:3], -0.5 + 2.0 ** -9, op.mult, op.add))
-    wait("V", c_z)
-    c_zj = sig(V.tensor_scalar(T.zedj[:], T.zed[:], EIGHTH, None, op.mult))
-    wait("V", d_bq)
-    d_u = event()
-    for bh in range(2):
-        sig(V.tensor_scalar(T.uu[:, bh:64:2], T.n32[:], T.s0[:, 0:1], T.bq[:, bh:bh + 1], op.mult, op.add), d_u)
-    wait("V", g_c)
-    c_slj = sig(V.tensor_scalar(T.selj[:], T.ioc[:], T.pf[:, 1:2], EIGHTH, op.is_equal, op.mult))
-    wait("V", d_u)
-    d_f = sig(V.tensor_scalar(T.ff[:], T.uu[:], MAGIC, MAGIC + 3.0, op.add, op.subtract))
-    wait("V", d_paf, c_id)
-    d_dia = sig(V.tensor_scalar(T.diaga[0:8, :], T.ident[0:8, 0:8], T.paf[0:8, 1:2], None, op.mult))
-    c_sel = sig(V.tensor_scalar(T.sel[:], T.ioc[:], T.pf[:, 1:2], None, op.is_equal))
-    wait("V", c_w0)
-    c_w = sig(V.tensor_scalar(T.wsum[:, 112:128], T.ioa[:, 0:16], T.pf[:, 0:1], None, op.is_equal))
+    def cols(name, b0, b1):
+        if name in ("ja", "jb"):
+            return T[name][:, b0:b1, :, :]
+        if name == "tt":
+            return T.tt[:, b0 // 4, 2 * (b0 % 4):2 * (b0 % 4) + 2, :] if b1 == b0 + 1 else T.tt[:, b0 // 4:b1 // 4, :, :]
+        if name == "ss":
+            return T.ss[:, 16 * b0:16 * b1]
+        return T.yy[:, 512 * int(name[1]) + 16 * b0:512 * int(name[1]) + 16 * b1]
 
-    jb = [T.t0, T.t1, T.acc0, T.acc1]
-    tb = [T.t2, T.t3, T.t0, T.t1]
-    blk = [slice(512 * i, 512 * (i + 1)) for i in range(4)]
-    e_j, e_w, e_s, e_t, e_add, e_off = {}, {}, {}, {}, {}, {}
+    def unit(k, b):
+        if k == 3 and b >= 24:
+            return "tt", 24
+        return (("ja", "jb"), ("y2", "y3"), ("tt", "ss"), ("y0", "y1"))[k][b // 16], 16 * (b // 16)
 
-    def delays(bank, i, z):
-        rows = slice(32 * i, 32 * (i + 1))
-        P.matmul(bank[:], T.xd[rows, :, :], z[rows, :], True, False)
+    opened = set()
+    free.update({"ja": [e_sq[(1, 0)]], "jb": [e_sq[(1, 1)]], "tt": [e_off[1]],
+                 "y0": [e_pairs], "y1": [e_pairs], "y2": [e_pairs], "y3": [e_pairs]})
+    summed = {}
 
-    def folds(bank, i, s):
-        rows = slice(32 * i, 32 * (i + 1))
-        for m in range(8):
-            gl = m // 4
-            mm = P.matmul(bank[:, 64 * m:64 * (m + 1)], s[rows, 128 * gl:128 * (gl + 1)], T.ff[rows, :], False, False)
-        return mm
-
-    def make_j(i):
-        rows = slice(32 * i, 32 * (i + 1))
-        folds(jb[i], i, T.selj)
-        e_j[i] = sig(P.matmul(jb[i][:], T.big[rows, :], T.zed[rows, :], False, True))
-        wait("A", e_j[i])
-        e_w[i] = sig(A.activation(T.jw[:, blk[i]], jb[i][:], fn.Square, bias=-MAGIC))
-
-    def make_t(i):
-        e_t[i] = sig(folds(tb[i], i, T.sel))
-
-    def shift(i):
-        wait("V", p_s1, e_w[i])
-        e_s[i] = event()
-        for gl in range(2):
-            tr = 2 * i + gl
-            cols = slice(256 * tr, 256 * (tr + 1))
-            sig(V.tensor_scalar(T.sh[:, cols], T.jw[:, cols], T.s1[:, tr:tr + 1], 1535.5 + 2.0 ** -13,
-                                op.mult, op.add), e_s[i])
-
-    def add_shift(i):
-        wait("P", c_id, e_t[i], e_s[i])
-        e_add[i] = sig(P.matmul(tb[i][:], T.ident[:], T.sh[:, blk[i]], False, True))
-
-    def offsets(i):
-        wait("V", e_add[i])
-        e_off[i] = event()
-        for gl in range(2):
-            tr = 2 * i + gl
-            sig(V.tensor_scalar(T.off[:, :, 32 * tr:32 * (tr + 1)], tb[i][:, 256 * gl:256 * (gl + 1)], -1533.0, None,
-                                op.add), e_off[i])
-
-    wait("P", c_z, d_x)
-    delays(tb[0], 0, T.zed)
-    delays(tb[1], 1, T.zed)
-    wait("P", c_zj)
-    delays(jb[0], 0, T.zedj)
-    delays(jb[1], 1, T.zedj)
-    wait("P", c_slj, d_f, c_big)
-    make_j(0)
-    wait("P", c_two, d_dia)
-    p_s1 = sig(P.matmul(T.s1[:, 0:8], T.twos[0:8, :], T.diaga[0:8, :], True, True))
-    make_j(1)
-    wait("P", c_sel)
-    make_t(0)
-    delays(jb[2], 2, T.zedj)
-    make_j(2)
-    shift(0)
-    add_shift(0)
-    delays(jb[3], 3, T.zedj)
-    make_j(3)
-    make_t(1)
-    shift(1)
-    add_shift(1)
-    offsets(0)
-    delays(tb[2], 2, T.zed)
-    make_t(2)
-    shift(2)
-    add_shift(2)
-    offsets(1)
-    delays(tb[3], 3, T.zed)
-    make_t(3)
-    shift(3)
-    add_shift(3)
-    offsets(2)
-    offsets(3)
-
-    done = {}
-
-    def gather(q, ph, g0, g1):
-        wait(q, *ready[ph // 2])
-        wait(q, *[e_off[i] for i in range(g0 // 2, (g1 + 1) // 2)])
-        out = T.gat[:, 4096 * ph + 512 * g0:4096 * ph + 512 * g1]
-        picked = wins[ph // 2][:, 0:S].indirect(T.off[:, ph, 32 * g0:32 * g1])
+    def gather(q, k, b0, b1):
+        wait(q, e_pairs, lists[k], *copied)
+        lo = 4096 * k
+        tile = T.offl[:, 3, 8 * b0:8 * b1] if k == 3 else T.offr[:, k, 8 * b0:8 * b1]
+        out = T.gat[:, lo + 128 * b0:lo + 128 * b1]
+        picked = T.pairs[:, 0:NSTEP * S].indirect(tile)
         if q == "A":
-            done[(ph, g0)] = sig(A.activation(out, picked, fn.Copy))
+            ev = act(out, picked, fn.Identity, bias=-float(DROP[k]))
         else:
-            done[(ph, g0)] = sig(V.tensor_copy(out, picked))
+            ev = ts(out, picked, -float(DROP[k]), None, op.add)
+        return k, b0, b1, ev
 
-    acc = [T.acc0, T.acc1]
-    left = [32, 32]
-    full = {}
+    def start(k, b):
+        name, base = unit(k, b)
+        if (k, base) in opened:
+            return False
+        opened.add((k, base))
+        wait("P", *free[name])
+        return True
 
-    def add_up(ph, g0, g1):
-        wait("P", c_w, done[(ph, g0)])
-        kh = ph % 2
-        for tr in range(g0, g1):
-            lo = 4096 * ph + 512 * tr
-            mm = P.matmul(acc[kh][:], T.wsum[:, 112 - 16 * tr:240 - 16 * tr], T.gat[:, lo:lo + 512],
-                          left[kh] == 32, left[kh] == 1)
-            left[kh] -= 1
-        if left[kh] == 0:
-            full[kh] = sig(mm)
+    def add_up(piece, last=False):
+        k, b0, b1, ev = piece
+        wait("P", c_w, ev)
+        for b in range(b0, b1):
+            name, base = unit(k, b)
+            mm = P.matmul(cols(name, b - base, b - base + 1), T.gat[:, 4096 * k + 128 * b:4096 * k + 128 * (b + 1)],
+                          T.wsel[:], start(k, b), last and b == b1 - 1)
+        if last:
+            summed[(k, base)] = sig("P", mm)
 
-    clipped = {}
+    def split(high, low, k, b0, b1):
+        name = unit(k, b0)[0]
+        bank = cols(name, 0, b1 - b0)
+        wait("V", summed[(k, b0)])
+        eh = ts(high, bank, MAGIC, MAGIC, op.add, op.subtract)
+        wait("V", eh)
+        el = sig("V", V.tensor_tensor(low, bank, high, op.subtract))
+        free[name] = [el]
+        return eh, el
 
-    def clip(kh, lo, hi):
-        wait("V", full[kh])
-        clipped[(kh, lo)] = sig(V.tensor_scalar(T.clip[:, 512 * kh + lo:512 * kh + hi], acc[kh][:, lo:hi], 255.0, None,
-                                                op.min))
+    def send_part(i):
+        eh, el = split(T.outp[:, i, 0:256], T.outp[:, i, 256:512], i // 2, 16 * (i % 2), 16 * (i % 2) + 16)
+        wait("G", el)
+        send(i // 2, T.inp[:, i, :], T.outp[:, i, :], "part%d" % i, far)
 
-    def over_pulses(kh, lo, hi):
-        wait("P", clipped[(kh, lo)])
-        for c0 in range(512 * kh + lo, 512 * kh + hi, 32):
-            mm = P.matmul(T.s0[:, 0:32], T.ident[:], T.clip[:, c0:c0 + 32], c0 == 0, c0 == 1024 - 32)
+    def send_raw(h):
+        name = unit(2, 16 * h)[0]
+        at = slice(256 * h, 256 * (h + 1))
+        wait("A", summed[(2, 16 * h)])
+        ev = act(T.outr[:, at], cols(name, 0, 16), fn.Copy)
+        free[name] = [ev]
+        wait("G", ev)
+        send(2, T.inr[:, at], T.outr[:, at], "raw%d" % h, whole)
+
+    for i, nv in enumerate((8, 6, 7, 6, 7)):
+        k, b = i // 2, 16 * (i % 2)
+        pv, pa = gather("V", k, b, b + nv), gather("A", k, b + nv, b + 16)
+        add_up(pv)
+        if i:
+            send_part(i - 1)
+        add_up(pa, True)
+    for k, b in ((2, 16), (3, 0)):
+        pv, pa = gather("V", k, b, b + 9), gather("A", k, b + 9, b + 12)
+        add_up(pa)
+        send_raw(k - 2)
+        pa = gather("A", k, b + 12, b + 16)
+        add_up(pv)
+        add_up(pa, k == 2)
+
+    units = [(0, 16), (16, 24), (24, 32)]
+    even, odd = ("ja", "y2", "y0"), ("jb", "y3", "y1")
+    e_ev, e_od, e_ce, e_co = {}, {}, {}, {}
+
+    def add_raw(i, last):
+        b0, b1 = units[i]
+        wait("P", c_late, raws[b0 // 16])
+        mm = P.matmul(cols(unit(3, b0)[0], 0, b1 - b0), T.id32[:], T.inr[:, 16 * b0:16 * b1], start(3, b0), last)
+        if last:
+            summed[(3, b0)] = sig("P", mm)
+
+    def far_sums(i, banks, w, off):
+        b0, b1 = units[i]
+        lo, hi = off + 16 * (b0 % 16), off + 16 * (b0 % 16 + b1 - b0)
+        wait("P", parts[b0 // 16], parts[2 + b0 // 16], *free[banks[i]])
+        for k in range(2):
+            P.matmul(cols(banks[i], 0, b1 - b0), w[:], T.inp[:, 2 * k + b0 // 16, lo:hi], k == 0, False)
+
+    def own_sums(i):
+        b0, b1 = units[i]
+        high, low = T.hx[:, 16 * b0:16 * b1], T.hx[:, 512 + 16 * b0:512 + 16 * b1]
+        eh, el = split(high, low, 3, b0, b1)
+        far_sums(i, even, T.ident, 0)
+        far_sums(i, odd, T.id256, 256)
+        wait("P", eh)
+        e_ev[i] = sig("P", P.matmul(cols(even[i], 0, b1 - b0), T.ident[:], high, False, True))
+        wait("P", el)
+        e_od[i] = sig("P", P.matmul(cols(odd[i], 0, b1 - b0), T.id256[:], low, False, True))
+
+    def clip_even(q, i):
+        b0, b1 = units[i]
+        out, bank = T.cle[:, 16 * b0:16 * b1], cols(even[i], 0, b1 - b0)
+        wait(q, e_ev[i])
+        if q == "A":
+            e_ce[i] = act(out, bank, fn.Relu, bias=2.0, scale=-1.0), T.wneg
+        else:
+            e_ce[i] = ts(out, bank, 2.0, 0.0, op.subtract, op.min), T.wpos
+
+    def clip_odd(i):
+        b0, b1 = units[i]
+        wait("A", e_od[i])
+        e_co[i] = act(T.clo[:, 16 * b0:16 * b1], cols(odd[i], 0, b1 - b0), fn.Relu, bias=-105.0, scale=-1.0)
+
+    def over_pulses(i):
+        b0, b1 = units[i]
+        ev, w = e_ce[i]
+        wait("P", ev, *free["ss"])
+        for c0 in range(16 * b0, 16 * b1, 128):
+            P.matmul(T.ss[:, 0:32], T.cle[:, c0:c0 + 128], w[:, 1:33], c0 == 0, False)
+        wait("P", e_co[i])
+        for c0 in range(16 * b0, 16 * b1, 128):
+            mm = P.matmul(T.ss[:, 0:32], T.clo[:, c0:c0 + 128], T.wneg[:, 0:32], False, c0 == 384)
         return mm
 
-    pieces = [("A", 0, 0, 2), ("A", 1, 0, 4), ("V", 0, 2, 8), ("A", 1, 4, 8),
-              ("V", 2, 0, 8), ("A", 3, 0, 8),
-              ("V", 4, 0, 4), ("A", 5, 0, 4), ("V", 4, 4, 8), ("A", 5, 4, 8),
-              ("V", 6, 0, 4), ("A", 6, 4, 8),
-              ("V", 7, 0, 2), ("V", 7, 2, 3), ("A", 7, 4, 6)]
-    for q, ph, g0, g1 in pieces:
-        gather(q, ph, g0, g1)
-        add_up(ph, g0, g1)
-    clip(0, 0, 512)
-    over_pulses(0, 0, 512)
-    for q, ph, g0, g1 in [("A", 7, 6, 7), ("V", 7, 3, 4), ("A", 7, 7, 8)]:
-        gather(q, ph, g0, g1)
-        add_up(ph, g0, g1)
-    clip(1, 0, 256)
-    clip(1, 256, 512)
-    over_pulses(1, 0, 256)
-    p_y = sig(over_pulses(1, 256, 512))
-    wait("V", p_y)
-    v_y = sig(V.tensor_copy(T.yo[:], T.s0[:, 0:32]))
+    add_raw(0, True)
+    pv, pa = gather("V", 3, 16, 20), gather("A", 3, 20, 24)
+    add_up(pv)
+    add_up(pa)
+    own_sums(0)
+    add_raw(1, True)
+    add_raw(2, False)
+    pa = gather("A", 3, 24, 28)
+    add_up(pa)
+    pv = gather("V", 3, 30, 32)
+    clip_even("A", 0)
+    pa = gather("A", 3, 28, 30)
+    add_up(pv)
+    add_up(pa, True)
+    own_sums(1)
+    clip_odd(0)
+    own_sums(2)
+    over_pulses(0)
+    clip_even("A", 1)
+    clip_odd(1)
+    over_pulses(1)
+    clip_even("V", 2)
+    clip_odd(2)
+    p_out = sig("P", over_pulses(2))
+    wait("V", p_out)
+    v_y = ts(T.yo[:], T.ss[:, 0:32], 32 * 255.0, None, op.add)
     wait("Y", v_y)
-    stored = sig(Y.dma_start(T.y[:], T.yo[:]), n=16)
+    stored = sig("Y", Y.dma_start(T.y[:], T.yo[:]), n=16)
     wait("Y", stored)
+    g.wait_ge(T.sem.sent, sent[0])

import numpy as np
from concourse.bass import DstId, RemoteDMATransfer
from concourse.mybir import AluOpType, ActivationFunctionType

S = 2048
AMAX = 20
MAGIC = 12582912.0
LIFT = 1536.0
DROP = (2031, 2031, 2048, 2031)


def pair_spans():
    spans = {}
    t = np.arange(S)
    for a in range(-AMAX, AMAX + 1):
        s = t + ((a * (t >> 3) ** 2) >> 12)
        ok = (s >= 0) & (s < S)
        for df in range(3):
            both = ok[:S - df] & ok[df:]
            s0 = s[:S - df][both]
            d = s[df:][both] - s0
            for v in range(int(d.min()), int(d.max()) + 1):
                at = s0[d == v]
                if len(at):
                    lo, hi = spans.get(v, (S, 0))
                    spans[v] = (min(lo, int(at.min())), max(hi, int(at.max()) + 1))
    return spans


SPANS = pair_spans()
DMIN = min(SPANS)
NSTEP = max(SPANS) - DMIN + 1

SCRATCH = {
    "xs": ("sbuf", [128, S], "bfloat16"),
    "pairs": ("sbuf", [128, NSTEP * S], "float32"),
    "gat": ("sbuf", [128, 16384], "float16"),
    "offl": ("sbuf", [128, 4, 256], "uint16"),
    "offr": ("sbuf", [128, 3, 256], "uint16"),
    "outp": ("sbuf", [128, 4, 512], "float16"),
    "inp": ("sbuf", [128, 4, 512], "float16"),
    "outr": ("sbuf", [128, 512], "float32"),
    "inr": ("sbuf", [128, 512], "float32"),
    "hx": ("sbuf", [128, 1024], "float16"),
    "cle": ("sbuf", [128, 512], "float16"),
    "clo": ("sbuf", [128, 512], "float16"),
    "jw": ("sbuf", [128, 4, 16, 4, 8], "uint16"),
    "sh": ("sbuf", [128, 32, 8, 8], "float16"),
    "pai": ("sbuf", [128, 4], "int32"),
    "paf": ("sbuf", [128, 4], "float32"),
    "dei": ("sbuf", [128, 2], "int32"),
    "dfj": ("sbuf", [128, 2], "float32"),
    "pm": ("sbuf", [128, 8], "int32"),
    "pf": ("sbuf", [128, 8], "float32"),
    "ioa": ("sbuf", [128, 34], "bfloat16"),
    "iob": ("sbuf", [128, 64], "bfloat16"),
    "ioh": ("sbuf", [128, 128], "bfloat16"),
    "ioz": ("sbuf", [128, 128], "bfloat16"),
    "n32": ("sbuf", [128, 64], "float32"),
    "c256": ("sbuf", [128, 128], "bfloat16"),
    "fill": ("sbuf", [128, 3, 128], "float16"),
    "ident": ("sbuf", [128, 128], "float16"),
    "id256": ("sbuf", [128, 128], "bfloat16"),
    "id32": ("sbuf", [128, 128], "float32"),
    "ida": ("sbuf", [128, 128], "float16"),
    "idb": ("sbuf", [128, 128], "float16"),
    "e8": ("sbuf", [128, 128], "float32"),
    "sixteen": ("sbuf", [128, 128], "float32"),
    "big": ("sbuf", [128, 128], "bfloat16"),
    "diaga": ("sbuf", [128, 8], "float32"),
    "acol": ("sbuf", [128, 8], "float32"),
    "wabs": ("sbuf", [128, 33], "float16"),
    "wsel": ("sbuf", [128, 16], "float16"),
    "wpos": ("sbuf", [128, 33], "float16"),
    "wneg": ("sbuf", [128, 33], "float16"),
    "sel": ("sbuf", [128, 4, 128], "float16"),
    "sela": ("sbuf", [128, 4, 128], "float16"),
    "zed": ("sbuf", [128, 4, 128], "float16"),
    "zedt": ("sbuf", [128, 4, 128], "float16"),
    "xdj": ("sbuf", [128, 4, 32], "float16"),
    "bcol": ("sbuf", [128, 2], "float32"),
    "bq": ("sbuf", [128, 2], "float32"),
    "uu": ("sbuf", [128, 128], "float32"),
    "ffj": ("sbuf", [128, 128], "float16"),
    "yo": ("sbuf", [128, 32], "float32"),
    "yy": ("psum", [128, 2048], "float32"),
    "ja": ("psum", [128, 32, 2, 8], "float32"),
    "jb": ("psum", [128, 32, 2, 8], "float32"),
    "tt": ("psum", [128, 8, 8, 8], "float32"),
    "ss": ("psum", [128, 512], "float32"),
}
NEV = 140
SEMAPHORES = (["list0", "list1", "list2", "part0", "part1", "part2", "part3", "raw0", "raw1", "sent"]
              + ["e%d" % i for i in range(NEV)])


def bits(m):
    return bin(m).count("1")


def rank_program(g, core, T, topo):
    rank = T.rank_of(core)
    if rank is None:
        return
    op = AluOpType
    fn = ActivationFunctionType
    V, A, P, Y = g.vector, g.scalar, g.tensor, g.sync
    queues = {"G": g, "V": V, "A": A, "P": P, "Y": Y}

    others = [c for c in T.cores if c != core]
    sib = [c for c in others if c in topo.cores_of(core)][0]
    peer = [c for c in others if c != sib and topo.die(c) == topo.die(core)][0]
    diag = [c for c in others if c != sib and c != peer][0]
    partner = [diag, peer, sib, core]
    src = [T.rank_of(c) for c in partner]

    count = [0]
    known = {q: set() for q in queues}

    def event():
        ev = ["e%d" % count[0], 0, set()]
        count[0] += 1
        return ev

    def sig(q, inst, ev=None, n=1):
        if ev is None:
            ev = event()
        inst.then_inc(T.sem[ev[0]], n)
        ev[1] += n
        ev[2].update(known[q])
        return ev

    def wait(q, *evs):
        for ev in evs:
            if ev[0] not in known[q]:
                queues[q].wait_ge(T.sem[ev[0]], ev[1])
                known[q].add(ev[0])
                known[q].update(ev[2])

    def ts(out, in0, s1, s2, op0, op1=None, ev=None):
        if op1 is None:
            return sig("V", V.tensor_scalar(out, in0, s1, None, op0), ev)
        return sig("V", V.tensor_scalar(out, in0, s1, s2, op0, op1), ev)

    def act(out, in_, func, ev=None, **kw):
        return sig("A", A.activation(out, in_, func, **kw), ev)

    l_pa = sig("Y", Y.dma_start(T.pai[0:8, 0:2], T.pa[:]), n=16)
    l_de = sig("A", A.dma_start(T.dei[:], T.de[:]), n=16)
    l_x = event()
    for c in range(8):
        q = "Y" if c % 2 == 0 else "A"
        sig(q, queues[q].dma_start(T.xs[16 * c:16 * c + 16, :], T.x[:, S * c:S * (c + 1)]), l_x, 16)

    c_16 = sig("V", V.memset(T.sixteen[0:8, :], 16.0))
    c_256 = sig("V", V.memset(T.c256[:], 256.0))
    c_big = sig("V", V.memset(T.big[:], MAGIC / 4))
    kw = {"allow_small_or_imprecise_dtypes": True}
    g_p = sig("G", g.iota(T.pm[:, 4:5], [[0, 1]], 0, 1))
    g_h = sig("G", g.iota(T.ioh[:], [[0, 8], [1, 16]], 0, 0, **kw))
    g_a = sig("G", g.iota(T.ioa[:], [[1, 34]], 0, 0, **kw))
    wait("G", c_16)
    c_e8 = sig("G", g.affine_select(T.e8[0:8, :], T.sixteen[0:8, :], [[-1, 8], [0, 16]], op.is_equal, 0.0, 0, 1))
    g_z = sig("G", g.iota(T.ioz[:], [[0, 4], [16, 4], [0, 8]], 0, 0, **kw))
    g_b = sig("G", g.iota(T.iob[:], [[1, 4], [0, 16]], 0, 0, **kw))
    g_n = sig("G", g.iota(T.n32[:], [[0, 2], [32, 32]], 0, 0, **kw))
    wait("G", c_256)
    c_id256 = sig("G", g.affine_select(T.id256[:], T.c256[:], [[-1, 128]], op.is_equal, 0.0, 0, 1))

    wait("V", g_p)
    c_and = event()
    for k, m in enumerate((15, 63, 60, 3)):
        ts(T.pm[:, k:k + 1], T.pm[:, 4:5], m, None, op.bitwise_and, ev=c_and)
    wait("V", c_and)
    c_pf = sig("V", V.tensor_copy(T.pf[:, 0:5], T.pm[:, 0:5]))
    p15, p63, p60, p3, pall = [T.pf[:, k:k + 1] for k in range(5)]
    wait("V", c_pf, g_a)
    c_b1 = ts(T.bcol[:], T.ioa[:, 0:2], p15, p15, op.add, op.add)
    wait("V", g_h)
    c_sel = event()
    for k in range(4):
        ts(T.sel[:, k, :], T.ioh[:], 16.0 * k, p63, op.add, op.is_equal, c_sel)
    wait("V", g_z)
    c_z = event()

    def make_z(w):
        ts(T.zed[:, w, :], T.ioz[:], 4.0 * src[w], p60, op.add, op.is_equal, c_z)

    make_z(0)
    make_z(1)
    wait("V", l_pa)
    d_and = ts(T.pai[0:8, 2:4], T.pai[0:8, 0:2], 0x7FE0, None, op.bitwise_and)
    make_z(2)
    wait("V", d_and)
    d_paf = ts(T.paf[0:8, :], T.pai[0:8, :], 2.0 ** -20, None, op.mult)
    wait("P", c_e8, d_paf)
    p_s0 = sig("P", P.matmul(T.ss[:, 0:4], T.e8[0:8, :], T.paf[0:8, :], True, True))
    make_z(3)
    wait("V", l_de)
    d_dfj = ts(T.dfj[:], T.dei[:], -1023.5, 0.125, op.add, op.mult)
    wait("V", d_paf)
    d_dia = ts(T.diaga[0:8, :], T.ioa[0:8, 0:8], T.pf[0:8, 4:5], T.paf[0:8, 1:2], op.is_equal, op.mult)
    wait("V", p_s0, c_b1)
    d_bq = ts(T.bq[:], T.bcol[:], T.ss[:, 2:3], (-0.5 + 2.0 ** -9) / 8, op.mult, op.add)
    wait("V", d_dfj, g_b)
    d_xj = event()
    ts(T.xdj[:, :, 0:16], T.iob[:], p3, T.dfj[:, 0:1], op.is_equal, op.mult, d_xj)
    wait("V", d_bq, g_n)
    d_u = event()
    for e in range(2):
        ts(T.uu[:, 64 * e:64 * (e + 1)], T.n32[:], T.ss[:, 0:1], T.bq[:, e:e + 1], op.mult, op.add, d_u)
    ts(T.xdj[:, :, 16:32], T.iob[:], p3, T.dfj[:, 1:2], op.is_equal, op.mult, d_xj)
    wait("V", d_u)
    d_f = ts(T.ffj[:], T.uu[:], MAGIC / 8, MAGIC / 8 + 0.5, op.add, op.subtract)

    wait("A", c_256)
    c_fill = event()
    for k, v in enumerate((-2047.0 / 16384, 0.125, 1.0)):
        act(T.fill[:, k, :], T.c256[:], fn.Copy, c_fill, scale=v / 256)
    wait("A", c_b1)
    c_abs = act(T.wabs[:], T.ioa[:, 0:33], fn.Abs, bias=T.bcol[:, 1:2], scale=-1.0)
    wait("A", c_abs)
    c_pos = act(T.wpos[:], T.wabs[:], fn.Relu, bias=1.0, scale=-1.0)
    wait("A", c_pos)
    c_w = act(T.wsel[:], T.wpos[:, 1:33:2], fn.Copy, scale=1.0 / 256)
    act(T.wneg[:], T.wpos[:], fn.Copy, c_w, scale=-1.0)
    wait("A", c_sel)
    c_t = act(T.sela[:], T.sel[:], fn.Copy, scale=-2047.0 / 2048)
    wait("A", c_z)
    act(T.zedt[:], T.zed[:], fn.Copy, c_t, scale=2.0 ** -11)
    wait("G", c_fill)
    c_ab, c_late = event(), event()
    for out, k, ev in ((T.ida, 0, c_ab), (T.idb, 1, c_ab), (T.ident, 2, c_late), (T.id32, 2, c_late)):
        sig("G", g.affine_select(out[:], T.fill[:, k, :], [[-1, 128]], op.is_equal, 0.0, 0, 1), ev)

    wait("P", d_dia)
    p_s1 = sig("P", P.matmul(T.tt[:, 0, 0, :], T.sixteen[0:8, :], T.diaga[0:8, :], True, True))
    p_y = {}

    def make_y(k):
        wait("P", l_x, c_id256)
        p_y[k] = sig("P", P.matmul(T.yy[:, 512 * k:512 * (k + 1)], T.id256[:], T.xs[:, 512 * k:512 * (k + 1)],
                                   True, True))

    e_pairs = event()
    free = {"ss": [d_u]}

    def pairs_v(d, lo, hi):
        wait("V", *[p_y[k] for k in range(lo // 512, (hi + 511) // 512)])
        base = (d - DMIN) * S
        sig("V", V.tensor_tensor(T.pairs[:, base + lo:base + hi], T.yy[:, lo:hi], T.xs[:, lo + d:hi + d], op.add),
            e_pairs)

    def pairs_a(lo, hi):
        wait("A", l_x)
        act(T.pairs[:, -DMIN * S + lo:-DMIN * S + hi], T.xs[:, lo:hi], fn.Copy, e_pairs, scale=257.0)

    def pairs_p(d, lo, hi):
        wait("P", c_late, *free["ss"])
        P.matmul(T.ss[:, 0:hi - lo], T.id256[:], T.xs[:, lo:hi], True, False)
        return d, lo, hi, sig("P", P.matmul(T.ss[:, 0:hi - lo], T.ident[:], T.xs[:, lo + d:hi + d], False, True))

    copied = []

    def pairs_copy(d, lo, hi, ev):
        wait("A", ev)
        base = (d - DMIN) * S
        copied.append(act(T.pairs[:, base + lo:base + hi], T.ss[:, 0:hi - lo], fn.Copy))
        free["ss"] = [copied[-1]]

    jbank = [T.ja, T.jb]
    e_j, e_sq, e_sh, e_t, e_add, e_off = {}, {}, {}, {}, {}, {}

    def make_j(u, hh):
        rows = slice(64 * hh, 64 * (hh + 1))
        bank = jbank[hh]
        z = T.zed[rows, 2 * u:2 * u + 2, :]
        wait("P", c_z, d_xj)
        if u:
            wait("P", e_sq[(0, hh)])
        for e in range(2):
            P.matmul(bank[:, 16 * e:16 * (e + 1), :, :], T.xdj[rows, :, :], z, e == 0, False)
        wait("P", c_sel, d_f, c_big)
        for k in range(4):
            P.matmul(bank[:, k // 2:32:2, k % 2, :], T.sel[rows, k, :], T.ffj[rows, :], False, False)
        for e in range(2):
            mm = P.matmul(bank[:, 16 * e:16 * (e + 1), :, :], T.big[rows, :], z, False, e == 1)
        e_j[(u, hh)] = sig("P", mm)

    def make_t(u, hh):
        rows = slice(64 * hh, 64 * (hh + 1))
        wait("P", c_t, e_off[0] if u else c_a)
        if hh:
            wait("P", e_t[(u, 0)])
        P.matmul(T.tt[:, :, 4 * hh:4 * hh + 4, :], T.xdj[rows, :, :], T.zedt[rows, 2 * u:2 * u + 2, :], hh == 0, False)
        for k in range(4):
            for e, s in enumerate((T.sela, T.sel)):
                mm = P.matmul(T.tt[:, :, 4 * hh + k, :], s[rows, k, :], T.ffj[rows, 64 * e:64 * (e + 1)], False, False)
        e_t[(u, hh)] = sig("P", mm)

    def square(u, hh):
        wait("A", e_j[(u, hh)])
        e_sq[(u, hh)] = act(T.jw[:, 2 * u + hh, :, :, :], jbank[hh][:], fn.Square, bias=128.0 - MAGIC)

    def shift(q, u, hh):
        wait(q, c_a, e_sq[(u, hh)])
        if u not in e_sh:
            e_sh[u] = event()
        for k in range(4):
            tr = 4 * hh + k
            out, w, a = T.sh[:, 16 * u:16 * (u + 1), tr, :], T.jw[:, 2 * u + hh, :, k, :], T.acol[:, tr:tr + 1]
            if q == "A":
                act(out, w, fn.Identity, e_sh[u], bias=LIFT - 0.5 + 2.0 ** -13, scale=a)
            else:
                ts(out, w, a, LIFT - 0.5 + 2.0 ** -13, op.mult, op.add, e_sh[u])

    def add_shift(u):
        wait("P", c_ab, e_t[(u, 1)], e_sh[u])
        P.matmul(T.tt[:], T.ida[:], T.sh[:, 16 * u:16 * u + 8, :, :], False, False)
        e_add[u] = sig("P", P.matmul(T.tt[:], T.idb[:], T.sh[:, 16 * u + 8:16 * u + 16, :, :], False, True))

    def offsets(u):
        wait("A", e_add[u])
        e_off[u] = act(T.offl[:, 2 * u:2 * u + 2, :], T.tt[:], fn.Identity, bias=-DMIN * S + 1027.5 - LIFT,
                       scale=16384.0)

    lo1, hi1 = SPANS[-1]
    wait("A", p_s1)
    c_a = act(T.acol[:], T.tt[:, 0, 0, :], fn.Copy, scale=16.0)
    pairs_a(0, 1280)
    make_y(0)
    make_y(1)
    make_j(0, 0)
    make_j(0, 1)
    pairs_v(1, 0, 1024)
    pairs_v(2, 0, 448)
    square(0, 0)
    square(0, 1)
    make_t(0, 0)
    make_t(0, 1)
    make_y(2)
    make_y(3)
    shift("V", 0, 0)
    shift("A", 0, 1)
    add_shift(0)
    make_j(1, 0)
    make_j(1, 1)
    pairs_v(2, 448, 1024)
    pairs_v(3, SPANS[3][0], 1024)
    for d in sorted(SPANS):
        if d not in (0, -1):
            pairs_v(d, 1024 if d in (1, 2, 3) else SPANS[d][0], SPANS[d][1])
    pairs_v(-1, lo1 + 1008, hi1)
    pairs_a(1280, S)
    offsets(0)
    staged = pairs_p(-1, lo1, lo1 + 512)
    square(1, 0)
    shift("A", 1, 0)
    square(1, 1)
    make_t(1, 0)
    make_t(1, 1)
    pairs_copy(*staged)
    staged = pairs_p(-1, lo1 + 512, lo1 + 1008)
    shift("A", 1, 1)
    add_shift(1)
    pairs_copy(*staged)
    offsets(1)

    far = topo.mask(core, peer)
    whole = topo.mask(core, sib)
    near = whole & ~far
    sent = [0]

    def send(k, dst, source, sem, mask):
        r, p = topo.addr(partner[k], core)
        g.remote_dma(dst, source, T.sem[sem], T.sem.sent, p, r, mask)
        sent[0] += bits(mask)

    for k, mask in enumerate((far, far, near)):
        wait("G", e_off[k // 2])
        send(k, T.offr[:, k, :], T.offl[:, k, :], "list%d" % k, mask)
    lists = [["list0", bits(far), set()], ["list1", bits(far), set()], ["list2", bits(near), set()], e_off[1]]
    parts = [["part%d" % i, bits(far), set()] for i in range(4)]
    raws = [["raw%d" % k, bits(whole), set()] for k in range(2)]

    def cols(name, b0, b1):
        if name in ("ja", "jb"):
            return T[name][:, b0:b1, :, :]
        if name == "tt":
            return T.tt[:, b0 // 4, 2 * (b0 % 4):2 * (b0 % 4) + 2, :] if b1 == b0 + 1 else T.tt[:, b0 // 4:b1 // 4, :, :]
        if name == "ss":
            return T.ss[:, 16 * b0:16 * b1]
        return T.yy[:, 512 * int(name[1]) + 16 * b0:512 * int(name[1]) + 16 * b1]

    def unit(k, b):
        if k == 3 and b >= 24:
            return "tt", 24
        return (("ja", "jb"), ("y2", "y3"), ("tt", "ss"), ("y0", "y1"))[k][b // 16], 16 * (b // 16)

    opened = set()
    free.update({"ja": [e_sq[(1, 0)]], "jb": [e_sq[(1, 1)]], "tt": [e_off[1]],
                 "y0": [e_pairs], "y1": [e_pairs], "y2": [e_pairs], "y3": [e_pairs]})
    summed = {}

    def gather(q, k, b0, b1):
        wait(q, e_pairs, lists[k], *copied)
        lo = 4096 * k
        tile = T.offl[:, 3, 8 * b0:8 * b1] if k == 3 else T.offr[:, k, 8 * b0:8 * b1]
        out = T.gat[:, lo + 128 * b0:lo + 128 * b1]
        picked = T.pairs[:, 0:NSTEP * S].indirect(tile)
        if q == "A":
            ev = act(out, picked, fn.Identity, bias=-float(DROP[k]))
        else:
            ev = ts(out, picked, -float(DROP[k]), None, op.add)
        return k, b0, b1, ev

    def start(k, b):
        name, base = unit(k, b)
        if (k, base) in opened:
            return False
        opened.add((k, base))
        wait("P", *free[name])
        return True

    def add_up(piece, last=False):
        k, b0, b1, ev = piece
        wait("P", c_w, ev)
        for b in range(b0, b1):
            name, base = unit(k, b)
            mm = P.matmul(cols(name, b - base, b - base + 1), T.gat[:, 4096 * k + 128 * b:4096 * k + 128 * (b + 1)],
                          T.wsel[:], start(k, b), last and b == b1 - 1)
        if last:
            summed[(k, base)] = sig("P", mm)

    def split(high, low, k, b0, b1):
        name = unit(k, b0)[0]
        bank = cols(name, 0, b1 - b0)
        wait("V", summed[(k, b0)])
        eh = ts(high, bank, MAGIC, MAGIC, op.add, op.subtract)
        wait("V", eh)
        el = sig("V", V.tensor_tensor(low, bank, high, op.subtract))
        free[name] = [el]
        return eh, el

    def send_part(i):
        eh, el = split(T.outp[:, i, 0:256], T.outp[:, i, 256:512], i // 2, 16 * (i % 2), 16 * (i % 2) + 16)
        wait("G", el)
        send(i // 2, T.inp[:, i, :], T.outp[:, i, :], "part%d" % i, far)

    def send_raw(h):
        name = unit(2, 16 * h)[0]
        at = slice(256 * h, 256 * (h + 1))
        wait("A", summed[(2, 16 * h)])
        ev = act(T.outr[:, at], cols(name, 0, 16), fn.Copy)
        free[name] = [ev]
        wait("G", ev)
        send(2, T.inr[:, at], T.outr[:, at], "raw%d" % h, whole)

    for i, nv in enumerate((8, 6, 7, 6, 7)):
        k, b = i // 2, 16 * (i % 2)
        pv, pa = gather("V", k, b, b + nv), gather("A", k, b + nv, b + 16)
        add_up(pv)
        if i:
            send_part(i - 1)
        add_up(pa, True)
    for k, b in ((2, 16), (3, 0)):
        pv, pa = gather("V", k, b, b + 9), gather("A", k, b + 9, b + 12)
        add_up(pa)
        send_raw(k - 2)
        pa = gather("A", k, b + 12, b + 16)
        add_up(pv)
        add_up(pa, k == 2)

    units = [(0, 16), (16, 24), (24, 32)]
    even, odd = ("ja", "y2", "y0"), ("jb", "y3", "y1")
    e_ev, e_od, e_ce, e_co = {}, {}, {}, {}

    def add_raw(i, last):
        b0, b1 = units[i]
        wait("P", c_late, raws[b0 // 16])
        mm = P.matmul(cols(unit(3, b0)[0], 0, b1 - b0), T.id32[:], T.inr[:, 16 * b0:16 * b1], start(3, b0), last)
        if last:
            summed[(3, b0)] = sig("P", mm)

    def far_sums(i, banks, w, off):
        b0, b1 = units[i]
        lo, hi = off + 16 * (b0 % 16), off + 16 * (b0 % 16 + b1 - b0)
        wait("P", parts[b0 // 16], parts[2 + b0 // 16], *free[banks[i]])
        for k in range(2):
            P.matmul(cols(banks[i], 0, b1 - b0), w[:], T.inp[:, 2 * k + b0 // 16, lo:hi], k == 0, False)

    def own_sums(i):
        b0, b1 = units[i]
        high, low = T.hx[:, 16 * b0:16 * b1], T.hx[:, 512 + 16 * b0:512 + 16 * b1]
        eh, el = split(high, low, 3, b0, b1)
        far_sums(i, even, T.ident, 0)
        far_sums(i, odd, T.id256, 256)
        wait("P", eh)
        e_ev[i] = sig("P", P.matmul(cols(even[i], 0, b1 - b0), T.ident[:], high, False, True))
        wait("P", el)
        e_od[i] = sig("P", P.matmul(cols(odd[i], 0, b1 - b0), T.id256[:], low, False, True))

    def clip_even(q, i):
        b0, b1 = units[i]
        out, bank = T.cle[:, 16 * b0:16 * b1], cols(even[i], 0, b1 - b0)
        wait(q, e_ev[i])
        if q == "A":
            e_ce[i] = act(out, bank, fn.Relu, bias=2.0, scale=-1.0), T.wneg
        else:
            e_ce[i] = ts(out, bank, 2.0, 0.0, op.subtract, op.min), T.wpos

    def clip_odd(i):
        b0, b1 = units[i]
        wait("A", e_od[i])
        e_co[i] = act(T.clo[:, 16 * b0:16 * b1], cols(odd[i], 0, b1 - b0), fn.Relu, bias=-105.0, scale=-1.0)

    def over_pulses(i):
        b0, b1 = units[i]
        ev, w = e_ce[i]
        wait("P", ev, *free["ss"])
        for c0 in range(16 * b0, 16 * b1, 128):
            P.matmul(T.ss[:, 0:32], T.cle[:, c0:c0 + 128], w[:, 1:33], c0 == 0, False)
        wait("P", e_co[i])
        for c0 in range(16 * b0, 16 * b1, 128):
            mm = P.matmul(T.ss[:, 0:32], T.clo[:, c0:c0 + 128], T.wneg[:, 0:32], False, c0 == 384)
        return mm

    add_raw(0, True)
    pv, pa = gather("V", 3, 16, 20), gather("A", 3, 20, 24)
    add_up(pv)
    add_up(pa)
    own_sums(0)
    add_raw(1, True)
    add_raw(2, False)
    pa = gather("A", 3, 24, 28)
    add_up(pa)
    pv = gather("V", 3, 30, 32)
    clip_even("A", 0)
    pa = gather("A", 3, 28, 30)
    add_up(pv)
    add_up(pa, True)
    own_sums(1)
    clip_odd(0)
    own_sums(2)
    over_pulses(0)
    clip_even("A", 1)
    clip_odd(1)
    over_pulses(1)
    clip_even("V", 2)
    clip_odd(2)
    p_out = sig("P", over_pulses(2))
    wait("V", p_out)
    v_y = ts(T.yo[:], T.ss[:, 0:32], 32 * 255.0, None, op.add)
    wait("Y", v_y)
    stored = sig("Y", Y.dma_start(T.y[:], T.yo[:]), n=16)
    wait("Y", stored)
    g.wait_ge(T.sem.sent, sent[0])
